import numpy as np
import ml_dtypes


def mxq(x, axis, fmt="e4m3"):
    dtype, down = {"e4m3": (ml_dtypes.float8_e4m3fn, 7), "e5m2": (ml_dtypes.float8_e5m2, 14)}[fmt]
    v = np.moveaxis(np.asarray(x, np.float32).astype(ml_dtypes.bfloat16).astype(np.float64), axis, -1)
    blocks = v.reshape(v.shape[:-1] + (-1, 32))
    amax = np.abs(blocks).max(-1, keepdims=True)
    byte = np.maximum(np.where(amax > 0, np.frexp(amax)[1] - 1 + 127, 0) - down, 1)
    scale = np.exp2(byte - 127.0)
    codes = (blocks / scale).astype(np.float32).astype(dtype).astype(np.float64)
    return np.moveaxis((codes * scale).reshape(v.shape), -1, axis)


WIDE = False


def mx_kscale(k):
    if not WIDE:
        return np.ones(k)
    levels = np.array([10, -10, 5, -5, 0])
    if k % 512:
        return np.exp2(np.random.permutation(np.resize(levels, k // 32))).repeat(32)
    a = np.empty((k // 512, 16))
    for p in range(k // 512):
        a[p, :8] = np.random.permutation(np.resize(levels, 8))
        for g in range(8):
            far = levels[np.abs(levels - a[p, g]) >= 10]
            a[p, g + 8] = far[np.random.randint(len(far))]
    return np.exp2(a.ravel()).repeat(32)


BF16 = ml_dtypes.bfloat16


def bf(x):
    return np.asarray(x, np.float32).astype(BF16)


def f64(x):
    return np.asarray(x).astype(np.float64)


E2M1 = np.array([0.0, 0.5, 1.0, 1.5, 2.0, 3.0, 4.0, 6.0, -0.0, -0.5, -1.0, -1.5, -2.0, -3.0, -4.0, -6.0])


def pack_weight(w, fmt):
    k, n = w.shape
    w = f64(bf(w)).reshape(k // 32, 32, n)
    amax = np.abs(w).max(1)
    if fmt == "e4m3":
        byte = np.frexp(amax)[1] - 1 + 127 - 7
    else:
        mant, ex = np.frexp(amax / 6.0)
        byte = np.where(mant > 0.5, ex, ex - 1) + 127
    byte = np.clip(np.where(amax > 0, byte, 1), 1, 254)
    scaled = (w * np.exp2(127.0 - byte)[:, None, :]).reshape(k, n).astype(np.float32)
    by_word = np.ascontiguousarray(scaled.reshape(k // 512, 128, 4, n).transpose(0, 1, 3, 2))
    if fmt == "e4m3":
        words = by_word.astype(ml_dtypes.float8_e4m3fn).view(np.uint8)
    else:
        c = by_word.astype(ml_dtypes.float4_e2m1fn).view(np.uint8) & 0xF
        words = c[..., 0::2] | (c[..., 1::2] << 4)
    return np.ascontiguousarray(words), np.ascontiguousarray(byte.astype(np.uint8).reshape(k // 512, 16, n))


def unpack_weight(words, scales, fmt):
    g, p, n, _ = words.shape
    if fmt == "e4m3":
        vals = np.ascontiguousarray(words).view(ml_dtypes.float8_e4m3fn).astype(np.float64)
    else:
        nib = np.empty((g, p, n, 4), np.uint8)
        nib[..., 0::2] = words & 0xF
        nib[..., 1::2] = words >> 4
        vals = E2M1[nib]
    vals = vals * np.repeat(np.exp2(scales.astype(np.float64) - 127.0), 8, axis=1)[..., None]
    return vals.transpose(0, 1, 3, 2).reshape(g * 512, n)

def planes(Y):
    n, m = Y.shape
    b = f64(bf(Y)).reshape(n // 32, 32, m)
    amax = np.abs(b).max(1)
    byte = np.clip(np.where(amax > 0, np.frexp(amax)[1] - 1 + 127 - 7, 1), 1, 254)
    codes = (b * np.exp2(127.0 - byte)[:, None, :]).reshape(n, m).astype(np.float32).astype(ml_dtypes.float8_e4m3fn).view(np.uint8)
    words = codes.reshape(n // 512, 128, 4, m).transpose(0, 1, 3, 2)
    return np.ascontiguousarray(words), np.ascontiguousarray(byte.astype(np.uint8).reshape(n // 512, 16, m))


N, D, R, F = 1024, 1024, 512, 2048


def silu(t):
    return t / (1.0 + np.exp(-t))


def bottleneck(xq, a_words, a_scales, g, b_words, b_scales):
    h = silu(xq @ unpack_weight(a_words, a_scales, "e4m3")) * f64(g)[None, :]
    return mxq(h, 1, "e4m3") @ unpack_weight(b_words, b_scales, "e4m3")


def setup_inputs():
    s = mx_kscale(D)
    t, u = mx_kscale(R), mx_kscale(R)
    x = bf(np.random.standard_normal((N, D)) * s)
    a_gate_words, a_gate_scales = pack_weight(np.random.standard_normal((D, R)) * (1.5 / np.sqrt(D)) / s[:, None], "e4m3")
    a_up_words, a_up_scales = pack_weight(np.random.standard_normal((D, R)) * (1.5 / np.sqrt(D)) / s[:, None], "e4m3")
    gg = bf((1.0 + 0.1 * np.random.standard_normal(R)) * t)
    gu = bf((1.0 + 0.1 * np.random.standard_normal(R)) * u)
    b_gate_words, b_gate_scales = pack_weight(np.random.standard_normal((R, F)) * (1.5 / np.sqrt(R)) / t[:, None], "e4m3")
    b_up_words, b_up_scales = pack_weight(np.random.standard_normal((R, F)) * (1.5 / np.sqrt(R)) / u[:, None], "e4m3")
    return {
        "x": x,
        "a_gate_words": a_gate_words,
        "a_gate_scales": a_gate_scales,
        "a_up_words": a_up_words,
        "a_up_scales": a_up_scales,
        "gg": gg,
        "gu": gu,
        "b_gate_words": b_gate_words,
        "b_gate_scales": b_gate_scales,
        "b_up_words": b_up_words,
        "b_up_scales": b_up_scales,
    }


def core(x, a_gate_words, a_gate_scales, a_up_words, a_up_scales, gg, gu, b_gate_words, b_gate_scales, b_up_words, b_up_scales):
    xq = mxq(f64(x), 1, "e4m3")
    e = bottleneck(xq, a_gate_words, a_gate_scales, gg, b_gate_words, b_gate_scales)
    v = bottleneck(xq, a_up_words, a_up_scales, gu, b_up_words, b_up_scales)
    return silu(e) * v


def reference(x, a_gate_words, a_gate_scales, a_up_words, a_up_scales, gg, gu, b_gate_words, b_gate_scales, b_up_words, b_up_scales):
    R_out = core(x, a_gate_words, a_gate_scales, a_up_words, a_up_scales, gg, gu, b_gate_words, b_gate_scales, b_up_words, b_up_scales)
    words, scales = planes(R_out)
    return R_out, words, scales

@@ -1,0 +1,305 @@
+from contextlib import ExitStack
+
+import concourse.mybir as mybir
+from concourse.masks import make_identity
+
+N, D, R, F = 1024, 1024, 512, 2048
+FLOPS = 2 * 2 * (N * D * R + N * R * F)
+
+F32 = mybir.dt.float32
+BF16 = mybir.dt.bfloat16
+I32 = mybir.dt.int32
+U32 = mybir.dt.uint32
+U8 = mybir.dt.uint8
+FP8X4 = mybir.dt.float8_e4m3fn_x4
+SILU = mybir.ActivationFunctionType.Silu
+MULT = mybir.AluOpType.mult
+
+P = 128
+PACK = 4
+GATE, UP = 0, 1
+CHUNK = 512
+CHUNKS = F // CHUNK
+V_COLS = 256
+
+
+def tile_colabottleneckactivationglu_x2_kernel(
+    tc, x, a_gate_words, a_gate_scales, a_up_words, a_up_scales, gg, gu,
+    b_gate_words, b_gate_scales, b_up_words, b_up_scales, out, out_words, out_scales,
+):
+    nc = tc.nc
+    with ExitStack() as ctx:
+        keep = ctx.enter_context(tc.tile_pool(name="keep", bufs=1))
+        work = ctx.enter_context(tc.tile_pool(name="work", bufs=3))
+        psum = ctx.enter_context(tc.psum_pool(name="psum", bufs=4))
+        ctx.enter_context(tc.manual_schedule())
+
+        a_planes = keep.tile([P, R], U8, name="a_planes", align_bytes=64)
+        b_planes = keep.tile([P, F], U8, name="b_planes", align_bytes=64)
+        nc.vector.memset(a_planes[:].bitcast(I32), 0)
+        nc.vector.memset(b_planes[:].bitcast(I32), 0)
+        ident = keep.tile([P, P], F32, name="ident")
+        make_identity(nc, ident[:])
+
+        x_rows = [keep.tile([P, PACK, D], BF16, name="x_rows%d" % g) for g in range(2)]
+        a_raw = [keep.tile([P, 2, R], I32, name="a_raw%d" % br) for br in range(2)]
+        a_codes = [keep.tile([P, 2, R], I32, name="a_codes%d" % br, align_bytes=64) for br in range(2)]
+        a_scale = keep.tile([P, R], U8, name="a_scale", align_bytes=64)
+        b_codes = [keep.tile([P, F], I32, name="b_codes%d" % br, align_bytes=64) for br in range(2)]
+        gains = [keep.tile([P, PACK], BF16, name="gains%d" % br) for br in range(2)]
+        x_hbm = x.rearrange("(g p t) d -> g p t d", g=2, t=PACK)
+        a_words_hbm = [w.rearrange("g p n t -> p g (n t)").bitcast(I32) for w in (a_gate_words, a_up_words)]
+        b_words_hbm = [w[0].rearrange("p n t -> p (n t)").bitcast(I32) for w in (b_gate_words, b_up_words)]
+        a_scales_hbm = [s.bitcast(I32) for s in (a_gate_scales, a_up_scales)]
+        b_scales_hbm = [s[0].bitcast(I32) for s in (b_gate_scales, b_up_scales)]
+
+        def load_x(s):
+            nc.sync.dma_start(out=x_rows[s // 4][:, s % 4, :], in_=x_hbm[s // 4][:, s % 4, :])
+
+        def load_b(c, br):
+            cols = slice(c * CHUNK, (c + 1) * CHUNK)
+            nc.sync.dma_start(out=b_codes[br][:, cols], in_=b_words_hbm[br][:, cols])
+
+        def load_a_scales(queue, br):
+            for q in range(4):
+                lo = 32 * q + 8 * br
+                queue.dma_start(
+                    out=a_planes[lo : lo + 8, :].bitcast(I32),
+                    in_=a_scales_hbm[br][:, 4 * q : 4 * q + 4, :],
+                )
+
+        def load_b_scales(queue, br):
+            for q in range(4):
+                lo = 32 * q + 4 * br
+                queue.dma_start(
+                    out=b_planes[lo : lo + 4, :].bitcast(I32),
+                    in_=b_scales_hbm[br][4 * q : 4 * q + 4, :],
+                )
+
+        load_x(0)
+        load_a_scales(nc.sync, GATE)
+        load_a_scales(nc.gpsimd, UP)
+        load_b_scales(nc.gpsimd, GATE)
+        nc.sync.dma_start(out=a_raw[GATE][:], in_=a_words_hbm[GATE])
+        nc.sync.dma_start(out=a_raw[UP][:], in_=a_words_hbm[UP])
+        load_x(1)
+        nc.scalar.dma_start(out=gains[GATE][:], in_=gg.rearrange("(p j) -> p j", j=PACK))
+        nc.scalar.dma_start(out=gains[UP][:], in_=gu.rearrange("(p j) -> p j", j=PACK))
+        load_b(0, GATE)
+        load_b(0, UP)
+        load_b_scales(nc.sync, UP)
+        load_b(1, GATE)
+        load_b(1, UP)
+        load_x(2)
+        load_x(3)
+        for c in (2, 3):
+            load_b(c, GATE)
+            load_b(c, UP)
+        for s in range(4, 8):
+            load_x(s)
+
+        def order_channels(br):
+            nc.vector.tensor_copy(
+                out=a_codes[br][:].rearrange("p g (j m) -> p g m j", j=PACK),
+                in_=a_raw[br][:].rearrange("p g (m j) -> p g m j", j=PACK),
+            )
+
+        def order_scales():
+            nc.vector.tensor_copy(
+                out=a_scale[:].rearrange("p (j m) -> p m j", j=PACK),
+                in_=a_planes[:].rearrange("p (m j) -> p m j", j=PACK),
+            )
+
+        x_groups, x_codes, x_scale = {}, {}, {}
+        h_act, h_groups, h_codes, h_scale = {}, {}, {}, {}
+        v_bank, e_act = {}, {}
+        f_rows, o_groups, o_scale = {}, {}, {}
+        for g in range(2):
+            o_scale[g] = keep.tile([P, F], U8, name="o_scale%d" % g, align_bytes=64)
+        f_rows[0] = keep.tile([P, PACK, F], F32, name="f_rows0")
+
+        def turn(s):
+            words = x_rows[s // 4][:].rearrange("p t d -> p (t d)").bitcast(F32)
+            base = (s % 4) * (D // 2)
+            bank = psum.tile([P, 2, 2, P], F32, tag="s_bank", bufs=4, name="turned")
+            for c in range(2):
+                for u in range(2):
+                    lo = base + 256 * c + u
+                    nc.tensor.transpose(bank[:, c, u, :], words[:, lo : lo + 255 : 2], ident[:])
+            x_groups[s] = work.tile([P, 2, P, 2], F32, tag="x_group", bufs=3, name="x_group", align_bytes=64)
+            if s < 2:
+                nc.vector.tensor_copy(out=x_groups[s][:], in_=bank[:].rearrange("p c u r -> p c r u"))
+            else:
+                nc.scalar.copy(out=x_groups[s][:], in_=bank[:].rearrange("p c u r -> p c r u"))
+
+        def quantize_x(s):
+            x_codes[s] = work.tile([P, 2 * P], U32, tag="x_code", bufs=3, name="x_code", align_bytes=64)
+            x_scale[s] = work.tile([P, 2 * P], U8, tag="x_scale", bufs=3, name="x_scale", align_bytes=64)
+            nc.vector.quantize_mx(
+                out=x_codes[s][:].bitcast(FP8X4),
+                scales=x_scale[s][:],
+                in_=x_groups[s][:].rearrange("p c r u -> p (c r u)").bitcast(BF16),
+            )
+
+        def hidden(s, br):
+            bank = psum.tile([P, PACK, P], F32, tag="s_bank", bufs=4, name="z_bank")
+            for j in range(PACK):
+                for c in range(2):
+                    nc.tensor.matmul_mx(
+                        out=bank[:, j, :],
+                        lhsT=a_codes[br][:, c, P * j : P * j + P].bitcast(FP8X4),
+                        lhsT_scale=a_scale[8 * br + 4 * c : P, P * j : P * j + P],
+                        rhs=x_codes[s][:, P * c : P * c + P].bitcast(FP8X4),
+                        rhs_scale=x_scale[s][:, P * c : P * c + P],
+                        start=(c == 0),
+                        stop=(c == 1),
+                    )
+            h_act[s, br] = work.tile([P, PACK, P], F32, tag="h_act", bufs=4, name="h_act")
+            nc.scalar.activation(out=h_act[s, br][:], in_=bank[:], func=SILU)
+
+        def apply_gain(s, br):
+            h_groups[s, br] = work.tile([P, P, PACK], BF16, tag="h_group", bufs=4, name="h_group", align_bytes=64)
+            nc.vector.tensor_tensor(
+                out=h_groups[s, br][:].rearrange("p (b i) j -> p b j i", i=4),
+                in0=h_act[s, br][:].rearrange("p j (b i) -> p b j i", i=4),
+                in1=gains[br][:].unsqueeze(1).unsqueeze(3).to_broadcast([P, P // 4, PACK, 4]),
+                op=MULT,
+            )
+
+        def quantize_h(s, br):
+            h_codes[s, br] = keep.tile([P, P], U32, name="h_code%d_%d" % (s, br), align_bytes=64)
+            h_scale[s, br] = keep.tile([P, P], U8, name="h_scale%d_%d" % (s, br), align_bytes=64)
+            nc.vector.quantize_mx(
+                out=h_codes[s, br][:].bitcast(FP8X4),
+                scales=h_scale[s, br][:],
+                in_=h_groups[s, br][:].rearrange("p n j -> p (n j)"),
+            )
+
+        def expand(s, c):
+            cols = slice(c * CHUNK, (c + 1) * CHUNK)
+            e_bank = psum.tile([P, CHUNK], F32, tag="s_bank", bufs=4, name="e_bank")
+            v_bank[s, c] = psum.tile([P, CHUNK], F32, tag="v_bank", bufs=4, name="v_bank")
+            for br, bank in ((GATE, e_bank), (UP, v_bank[s, c])):
+                nc.tensor.matmul_mx(
+                    out=bank[:],
+                    lhsT=h_codes[s, br][:].bitcast(FP8X4),
+                    lhsT_scale=h_scale[s, br][:],
+                    rhs=b_codes[br][:, cols].bitcast(FP8X4),
+                    rhs_scale=b_planes[4 * br : P, cols],
+                    start=True,
+                    stop=True,
+                )
+            e_act[s, c] = work.tile([P, CHUNK], F32, tag="e_act", bufs=4, name="e_act")
+            nc.scalar.activation(out=e_act[s, c][:], in_=e_bank[:], func=SILU)
+
+        def result_part(g, c, t):
+            if g == 0:
+                return f_rows[0][:, t, c * CHUNK : (c + 1) * CHUNK]
+            return f_rows[1, c][:, t, :]
+
+        def gate(s, c):
+            g, t = s // 4, s % 4
+            if g == 1 and t == 0:
+                f_rows[1, c] = work.tile([P, PACK, CHUNK], F32, tag="f_rows1", bufs=4, name="f_rows1")
+            nc.vector.tensor_tensor(out=result_part(g, c, t), in0=v_bank[s, c][:], in1=e_act[s, c][:], op=MULT)
+
+        out_hbm = out.rearrange("(g p t) f -> g p t f", g=2, t=PACK)
+        out_words_hbm = out_words.rearrange("g p m t -> g p (m t)").bitcast(I32)
+        out_scales_hbm = out_scales.bitcast(I32)
+
+        def store_rows0(t, c, n):
+            cols = slice(c * CHUNK, (c + n) * CHUNK)
+            nc.sync.dma_start(out=out_hbm[0][:, t, cols], in_=f_rows[0][:, t, cols])
+
+        def store_rows1(c, t, n):
+            cols = slice(c * CHUNK, (c + 1) * CHUNK)
+            nc.sync.dma_start(out=out_hbm[1][:, t : t + n, cols], in_=f_rows[1, c][:, t : t + n, :])
+
+        def cast(g, c, engine, lo, hi):
+            if (g, c) not in o_groups:
+                o_groups[g, c] = work.tile([P, CHUNK, PACK], BF16, tag="o_group", bufs=3, name="o_group", align_bytes=64)
+            if g == 0:
+                src = f_rows[0][:, :, c * CHUNK + lo : c * CHUNK + hi]
+            else:
+                src = f_rows[1, c][:, :, lo:hi]
+            src = src.rearrange("p t (b i) -> p b t i", i=4)
+            dst = o_groups[g, c][:, lo:hi, :].rearrange("p (b i) t -> p b t i", i=4)
+            if engine == "v":
+                nc.vector.tensor_copy(out=dst, in_=src)
+            else:
+                nc.scalar.copy(out=dst, in_=src)
+
+        def pack(g, c, lo, hi):
+            codes = work.tile([P, hi - lo], U32, tag="o_code", bufs=3, name="o_code", align_bytes=64)
+            cols = slice(c * CHUNK + lo, c * CHUNK + hi)
+            nc.vector.quantize_mx(
+                out=codes[:].bitcast(FP8X4),
+                scales=o_scale[g][:, cols],
+                in_=o_groups[g, c][:, lo:hi, :].rearrange("p n t -> p (n t)"),
+            )
+            nc.sync.dma_start(out=out_words_hbm[g][:, cols], in_=codes[:].bitcast(I32))
+
+        def store_scales(g, lo, hi):
+            for q in range(4):
+                nc.sync.dma_start(
+                    out=out_scales_hbm[g, 4 * q : 4 * q + 4, lo // 4 : hi // 4],
+                    in_=o_scale[g][32 * q : 32 * q + 4, lo:hi].bitcast(I32),
+                )
+
+        turn(0)
+        quantize_x(0)
+        order_channels(GATE)
+        order_scales()
+        hidden(0, GATE)
+        turn(1)
+        order_channels(UP)
+        hidden(0, UP)
+        quantize_x(1)
+        apply_gain(0, GATE)
+        turn(2)
+        apply_gain(0, UP)
+        quantize_h(0, GATE)
+        quantize_h(0, UP)
+
+        jobs = [(s, br) for s in range(1, 8) for br in (GATE, UP)]
+        for i in range(16):
+            s, c = i // 4, i % 4
+            expand(s, c)
+            if i < len(jobs):
+                hidden(*jobs[i])
+            if i % 2 == 1 and i // 2 + 3 < 8:
+                turn(i // 2 + 3)
+            if 1 <= i <= len(jobs):
+                apply_gain(*jobs[i - 1])
+            if i % 2 == 0 and i // 2 + 2 < 8:
+                quantize_x(i // 2 + 2)
+            gate(s, c)
+            if 1 <= i <= len(jobs):
+                quantize_h(*jobs[i - 1])
+            if c % 2 == 1:
+                store_rows0(s, c - 1, 2)
+
+        for c in range(CHUNKS):
+            units = [(0, c)] + ([(1, c - 1)] if c else [])
+            for t in range(PACK):
+                expand(4 + t, c)
+                if t // 2 < len(units):
+                    u = units[t // 2]
+                    lo = V_COLS + (t % 2) * P
+                    cast(*u, "s", lo, lo + P)
+                    if t % 2 == 0:
+                        cast(*u, "v", 0, V_COLS)
+                gate(4 + t, c)
+                if t // 2 < len(units) and t % 2 == 1:
+                    pack(*u, 0, CHUNK)
+                if c < 3 and t % 2 == 1:
+                    store_rows1(c, t - 1, 2)
+                if c == 3:
+                    store_rows1(c, t, 1)
+        store_scales(0, 0, F)
+        store_scales(1, 0, 3 * CHUNK)
+        for lo in (0, 256):
+            cast(1, 3, "v", lo, lo + P)
+            cast(1, 3, "s", lo + P, lo + 2 * P)
+            pack(1, 3, lo, lo + 256)
+        store_scales(1, 3 * CHUNK, F)

@@ -34,17 +34,17 @@ def tile_colabottleneckactivationglu_x2_kernel(
         psum = ctx.enter_context(tc.psum_pool(name="psum", bufs=4))
         ctx.enter_context(tc.manual_schedule())
 
-        a_planes = keep.tile([P, R], U8, name="a_planes", align_bytes=64)
+        a_planes = [keep.tile([P, R], U8, name="a_planes%d" % br, align_bytes=64) for br in range(2)]
         b_planes = keep.tile([P, F], U8, name="b_planes", align_bytes=64)
-        nc.vector.memset(a_planes[:].bitcast(I32), 0)
+        nc.vector.memset(a_planes[GATE][:].bitcast(I32), 0)
+        nc.vector.memset(a_planes[UP][:].bitcast(I32), 0)
         nc.vector.memset(b_planes[:].bitcast(I32), 0)
         ident = keep.tile([P, P], F32, name="ident")
-        make_identity(nc, ident[:])
 
         x_rows = [keep.tile([P, PACK, D], BF16, name="x_rows%d" % g) for g in range(2)]
         a_raw = [keep.tile([P, 2, R], I32, name="a_raw%d" % br) for br in range(2)]
         a_codes = [keep.tile([P, 2, R], I32, name="a_codes%d" % br, align_bytes=64) for br in range(2)]
-        a_scale = keep.tile([P, R], U8, name="a_scale", align_bytes=64)
+        a_scale = [keep.tile([P, R], U8, name="a_scale%d" % br, align_bytes=64) for br in range(2)]
         b_codes = [keep.tile([P, F], I32, name="b_codes%d" % br, align_bytes=64) for br in range(2)]
         gains = [keep.tile([P, PACK], BF16, name="gains%d" % br) for br in range(2)]
         x_hbm = x.rearrange("(g p t) d -> g p t d", g=2, t=PACK)
@@ -62,9 +62,8 @@ def tile_colabottleneckactivationglu_x2_kernel(
 
         def load_a_scales(queue, br):
             for q in range(4):
-                lo = 32 * q + 8 * br
                 queue.dma_start(
-                    out=a_planes[lo : lo + 8, :].bitcast(I32),
+                    out=a_planes[br][32 * q : 32 * q + 8, :].bitcast(I32),
                     in_=a_scales_hbm[br][:, 4 * q : 4 * q + 4, :],
                 )
 
@@ -76,21 +75,22 @@ def tile_colabottleneckactivationglu_x2_kernel(
                     in_=b_scales_hbm[br][4 * q : 4 * q + 4, :],
                 )
 
+        nc.gpsimd.dma_start(out=a_raw[GATE][:], in_=a_words_hbm[GATE])
+        nc.gpsimd.dma_start(out=a_raw[UP][:], in_=a_words_hbm[UP])
+        make_identity(nc, ident[:])
+        load_b_scales(nc.gpsimd, GATE)
         load_x(0)
         load_a_scales(nc.sync, GATE)
-        load_a_scales(nc.gpsimd, UP)
-        load_b_scales(nc.gpsimd, GATE)
-        nc.sync.dma_start(out=a_raw[GATE][:], in_=a_words_hbm[GATE])
-        nc.sync.dma_start(out=a_raw[UP][:], in_=a_words_hbm[UP])
+        load_a_scales(nc.sync, UP)
+        nc.sync.dma_start(out=gains[GATE][:], in_=gg.rearrange("(p j) -> p j", j=PACK))
+        nc.sync.dma_start(out=gains[UP][:], in_=gu.rearrange("(p j) -> p j", j=PACK))
         load_x(1)
-        nc.scalar.dma_start(out=gains[GATE][:], in_=gg.rearrange("(p j) -> p j", j=PACK))
-        nc.scalar.dma_start(out=gains[UP][:], in_=gu.rearrange("(p j) -> p j", j=PACK))
+        load_x(2)
         load_b(0, GATE)
         load_b(0, UP)
         load_b_scales(nc.sync, UP)
         load_b(1, GATE)
         load_b(1, UP)
-        load_x(2)
         load_x(3)
         for c in (2, 3):
             load_b(c, GATE)
@@ -104,10 +104,10 @@ def tile_colabottleneckactivationglu_x2_kernel(
                 in_=a_raw[br][:].rearrange("p g (m j) -> p g m j", j=PACK),
             )
 
-        def order_scales():
+        def order_scales(br):
             nc.vector.tensor_copy(
-                out=a_scale[:].rearrange("p (j m) -> p m j", j=PACK),
-                in_=a_planes[:].rearrange("p (m j) -> p m j", j=PACK),
+                out=a_scale[br][:].rearrange("p (j m) -> p m j", j=PACK),
+                in_=a_planes[br][:].rearrange("p (m j) -> p m j", j=PACK),
             )
 
         x_groups, x_codes, x_scale = {}, {}, {}
@@ -127,7 +127,7 @@ def tile_colabottleneckactivationglu_x2_kernel(
                     lo = base + 256 * c + u
                     nc.tensor.transpose(bank[:, c, u, :], words[:, lo : lo + 255 : 2], ident[:])
             x_groups[s] = work.tile([P, 2, P, 2], F32, tag="x_group", bufs=3, name="x_group", align_bytes=64)
-            if s < 2:
+            if s == 0:
                 nc.vector.tensor_copy(out=x_groups[s][:], in_=bank[:].rearrange("p c u r -> p c r u"))
             else:
                 nc.scalar.copy(out=x_groups[s][:], in_=bank[:].rearrange("p c u r -> p c r u"))
@@ -148,7 +148,7 @@ def tile_colabottleneckactivationglu_x2_kernel(
                     nc.tensor.matmul_mx(
                         out=bank[:, j, :],
                         lhsT=a_codes[br][:, c, P * j : P * j + P].bitcast(FP8X4),
-                        lhsT_scale=a_scale[8 * br + 4 * c : P, P * j : P * j + P],
+                        lhsT_scale=a_scale[br][4 * c : P, P * j : P * j + P],
                         rhs=x_codes[s][:, P * c : P * c + P].bitcast(FP8X4),
                         rhs_scale=x_scale[s][:, P * c : P * c + P],
                         start=(c == 0),
@@ -160,9 +160,9 @@ def tile_colabottleneckactivationglu_x2_kernel(
         def apply_gain(s, br):
             h_groups[s, br] = work.tile([P, P, PACK], BF16, tag="h_group", bufs=4, name="h_group", align_bytes=64)
             nc.vector.tensor_tensor(
-                out=h_groups[s, br][:].rearrange("p (b i) j -> p b j i", i=4),
-                in0=h_act[s, br][:].rearrange("p j (b i) -> p b j i", i=4),
-                in1=gains[br][:].unsqueeze(1).unsqueeze(3).to_broadcast([P, P // 4, PACK, 4]),
+                out=h_groups[s, br][:],
+                in0=h_act[s, br][:].rearrange("p j n -> p n j"),
+                in1=gains[br][:].unsqueeze(1).to_broadcast([P, P, PACK]),
                 op=MULT,
             )
 
@@ -222,8 +222,8 @@ def tile_colabottleneckactivationglu_x2_kernel(
                 src = f_rows[0][:, :, c * CHUNK + lo : c * CHUNK + hi]
             else:
                 src = f_rows[1, c][:, :, lo:hi]
-            src = src.rearrange("p t (b i) -> p b t i", i=4)
-            dst = o_groups[g, c][:, lo:hi, :].rearrange("p (b i) t -> p b t i", i=4)
+            src = src.rearrange("p t n -> p n t")
+            dst = o_groups[g, c][:, lo:hi, :]
             if engine == "v":
                 nc.vector.tensor_copy(out=dst, in_=src)
             else:
@@ -248,18 +248,19 @@ def tile_colabottleneckactivationglu_x2_kernel(
 
         turn(0)
         quantize_x(0)
+        order_scales(GATE)
         order_channels(GATE)
-        order_scales()
         hidden(0, GATE)
-        turn(1)
+        order_scales(UP)
         order_channels(UP)
         hidden(0, UP)
-        quantize_x(1)
         apply_gain(0, GATE)
-        turn(2)
-        apply_gain(0, UP)
+        turn(1)
         quantize_h(0, GATE)
+        apply_gain(0, UP)
+        turn(2)
         quantize_h(0, UP)
+        quantize_x(1)
 
         jobs = [(s, br) for s in range(1, 8) for br in (GATE, UP)]
         for i in range(16):
@@ -271,11 +272,11 @@ def tile_colabottleneckactivationglu_x2_kernel(
                 turn(i // 2 + 3)
             if 1 <= i <= len(jobs):
                 apply_gain(*jobs[i - 1])
-            if i % 2 == 0 and i // 2 + 2 < 8:
-                quantize_x(i // 2 + 2)
             gate(s, c)
             if 1 <= i <= len(jobs):
                 quantize_h(*jobs[i - 1])
+            if i % 2 == 0 and i // 2 + 2 < 8:
+                quantize_x(i // 2 + 2)
             if c % 2 == 1:
                 store_rows0(s, c - 1, 2)
 

from contextlib import ExitStack

import concourse.mybir as mybir
from concourse.masks import make_identity

N, D, R, F = 1024, 1024, 512, 2048
FLOPS = 2 * 2 * (N * D * R + N * R * F)

F32 = mybir.dt.float32
BF16 = mybir.dt.bfloat16
I32 = mybir.dt.int32
U32 = mybir.dt.uint32
U8 = mybir.dt.uint8
FP8X4 = mybir.dt.float8_e4m3fn_x4
SILU = mybir.ActivationFunctionType.Silu
MULT = mybir.AluOpType.mult

P = 128
PACK = 4
GATE, UP = 0, 1
CHUNK = 512
CHUNKS = F // CHUNK
V_COLS = 256


def tile_colabottleneckactivationglu_x2_kernel(
    tc, x, a_gate_words, a_gate_scales, a_up_words, a_up_scales, gg, gu,
    b_gate_words, b_gate_scales, b_up_words, b_up_scales, out, out_words, out_scales,
):
    nc = tc.nc
    with ExitStack() as ctx:
        keep = ctx.enter_context(tc.tile_pool(name="keep", bufs=1))
        work = ctx.enter_context(tc.tile_pool(name="work", bufs=3))
        psum = ctx.enter_context(tc.psum_pool(name="psum", bufs=4))
        ctx.enter_context(tc.manual_schedule())

        a_planes = [keep.tile([P, R], U8, name="a_planes%d" % br, align_bytes=64) for br in range(2)]
        b_planes = keep.tile([P, F], U8, name="b_planes", align_bytes=64)
        nc.vector.memset(a_planes[GATE][:].bitcast(I32), 0)
        nc.vector.memset(a_planes[UP][:].bitcast(I32), 0)
        nc.vector.memset(b_planes[:].bitcast(I32), 0)
        ident = keep.tile([P, P], F32, name="ident")

        x_rows = [keep.tile([P, PACK, D], BF16, name="x_rows%d" % g) for g in range(2)]
        a_raw = [keep.tile([P, 2, R], I32, name="a_raw%d" % br) for br in range(2)]
        a_codes = [keep.tile([P, 2, R], I32, name="a_codes%d" % br, align_bytes=64) for br in range(2)]
        a_scale = [keep.tile([P, R], U8, name="a_scale%d" % br, align_bytes=64) for br in range(2)]
        b_codes = [keep.tile([P, F], I32, name="b_codes%d" % br, align_bytes=64) for br in range(2)]
        gains = [keep.tile([P, PACK], BF16, name="gains%d" % br) for br in range(2)]
        x_hbm = x.rearrange("(g p t) d -> g p t d", g=2, t=PACK)
        a_words_hbm = [w.rearrange("g p n t -> p g (n t)").bitcast(I32) for w in (a_gate_words, a_up_words)]
        b_words_hbm = [w[0].rearrange("p n t -> p (n t)").bitcast(I32) for w in (b_gate_words, b_up_words)]
        a_scales_hbm = [s.bitcast(I32) for s in (a_gate_scales, a_up_scales)]
        b_scales_hbm = [s[0].bitcast(I32) for s in (b_gate_scales, b_up_scales)]

        def load_x(s):
            nc.sync.dma_start(out=x_rows[s // 4][:, s % 4, :], in_=x_hbm[s // 4][:, s % 4, :])

        def load_b(c, br):
            cols = slice(c * CHUNK, (c + 1) * CHUNK)
            nc.sync.dma_start(out=b_codes[br][:, cols], in_=b_words_hbm[br][:, cols])

        def load_a_scales(queue, br):
            for q in range(4):
                queue.dma_start(
                    out=a_planes[br][32 * q : 32 * q + 8, :].bitcast(I32),
                    in_=a_scales_hbm[br][:, 4 * q : 4 * q + 4, :],
                )

        def load_b_scales(queue, br):
            for q in range(4):
                lo = 32 * q + 4 * br
                queue.dma_start(
                    out=b_planes[lo : lo + 4, :].bitcast(I32),
                    in_=b_scales_hbm[br][4 * q : 4 * q + 4, :],
                )

        nc.gpsimd.dma_start(out=a_raw[GATE][:], in_=a_words_hbm[GATE])
        nc.gpsimd.dma_start(out=a_raw[UP][:], in_=a_words_hbm[UP])
        make_identity(nc, ident[:])
        load_b_scales(nc.gpsimd, GATE)
        load_x(0)
        load_a_scales(nc.sync, GATE)
        load_a_scales(nc.sync, UP)
        nc.sync.dma_start(out=gains[GATE][:], in_=gg.rearrange("(p j) -> p j", j=PACK))
        nc.sync.dma_start(out=gains[UP][:], in_=gu.rearrange("(p j) -> p j", j=PACK))
        load_x(1)
        load_x(2)
        load_b(0, GATE)
        load_b(0, UP)
        load_b_scales(nc.sync, UP)
        load_b(1, GATE)
        load_b(1, UP)
        load_x(3)
        for c in (2, 3):
            load_b(c, GATE)
            load_b(c, UP)
        for s in range(4, 8):
            load_x(s)

        def order_channels(br):
            nc.vector.tensor_copy(
                out=a_codes[br][:].rearrange("p g (j m) -> p g m j", j=PACK),
                in_=a_raw[br][:].rearrange("p g (m j) -> p g m j", j=PACK),
            )

        def order_scales(br):
            nc.vector.tensor_copy(
                out=a_scale[br][:].rearrange("p (j m) -> p m j", j=PACK),
                in_=a_planes[br][:].rearrange("p (m j) -> p m j", j=PACK),
            )

        x_groups, x_codes, x_scale = {}, {}, {}
        h_act, h_groups, h_codes, h_scale = {}, {}, {}, {}
        v_bank, e_act = {}, {}
        f_rows, o_groups, o_scale = {}, {}, {}
        for g in range(2):
            o_scale[g] = keep.tile([P, F], U8, name="o_scale%d" % g, align_bytes=64)
        f_rows[0] = keep.tile([P, PACK, F], F32, name="f_rows0")

        def turn(s):
            words = x_rows[s // 4][:].rearrange("p t d -> p (t d)").bitcast(F32)
            base = (s % 4) * (D // 2)
            bank = psum.tile([P, 2, 2, P], F32, tag="s_bank", bufs=4, name="turned")
            for c in range(2):
                for u in range(2):
                    lo = base + 256 * c + u
                    nc.tensor.transpose(bank[:, c, u, :], words[:, lo : lo + 255 : 2], ident[:])
            x_groups[s] = work.tile([P, 2, P, 2], F32, tag="x_group", bufs=3, name="x_group", align_bytes=64)
            if s == 0:
                nc.vector.tensor_copy(out=x_groups[s][:], in_=bank[:].rearrange("p c u r -> p c r u"))
            else:
                nc.scalar.copy(out=x_groups[s][:], in_=bank[:].rearrange("p c u r -> p c r u"))

        def quantize_x(s):
            x_codes[s] = work.tile([P, 2 * P], U32, tag="x_code", bufs=3, name="x_code", align_bytes=64)
            x_scale[s] = work.tile([P, 2 * P], U8, tag="x_scale", bufs=3, name="x_scale", align_bytes=64)
            nc.vector.quantize_mx(
                out=x_codes[s][:].bitcast(FP8X4),
                scales=x_scale[s][:],
                in_=x_groups[s][:].rearrange("p c r u -> p (c r u)").bitcast(BF16),
            )

        def hidden(s, br):
            bank = psum.tile([P, PACK, P], F32, tag="s_bank", bufs=4, name="z_bank")
            for j in range(PACK):
                for c in range(2):
                    nc.tensor.matmul_mx(
                        out=bank[:, j, :],
                        lhsT=a_codes[br][:, c, P * j : P * j + P].bitcast(FP8X4),
                        lhsT_scale=a_scale[br][4 * c : P, P * j : P * j + P],
                        rhs=x_codes[s][:, P * c : P * c + P].bitcast(FP8X4),
                        rhs_scale=x_scale[s][:, P * c : P * c + P],
                        start=(c == 0),
                        stop=(c == 1),
                    )
            h_act[s, br] = work.tile([P, PACK, P], F32, tag="h_act", bufs=4, name="h_act")
            nc.scalar.activation(out=h_act[s, br][:], in_=bank[:], func=SILU)

        def apply_gain(s, br):
            h_groups[s, br] = work.tile([P, P, PACK], BF16, tag="h_group", bufs=4, name="h_group", align_bytes=64)
            nc.vector.tensor_tensor(
                out=h_groups[s, br][:],
                in0=h_act[s, br][:].rearrange("p j n -> p n j"),
                in1=gains[br][:].unsqueeze(1).to_broadcast([P, P, PACK]),
                op=MULT,
            )

        def quantize_h(s, br):
            h_codes[s, br] = keep.tile([P, P], U32, name="h_code%d_%d" % (s, br), align_bytes=64)
            h_scale[s, br] = keep.tile([P, P], U8, name="h_scale%d_%d" % (s, br), align_bytes=64)
            nc.vector.quantize_mx(
                out=h_codes[s, br][:].bitcast(FP8X4),
                scales=h_scale[s, br][:],
                in_=h_groups[s, br][:].rearrange("p n j -> p (n j)"),
            )

        def expand(s, c):
            cols = slice(c * CHUNK, (c + 1) * CHUNK)
            e_bank = psum.tile([P, CHUNK], F32, tag="s_bank", bufs=4, name="e_bank")
            v_bank[s, c] = psum.tile([P, CHUNK], F32, tag="v_bank", bufs=4, name="v_bank")
            for br, bank in ((GATE, e_bank), (UP, v_bank[s, c])):
                nc.tensor.matmul_mx(
                    out=bank[:],
                    lhsT=h_codes[s, br][:].bitcast(FP8X4),
                    lhsT_scale=h_scale[s, br][:],
                    rhs=b_codes[br][:, cols].bitcast(FP8X4),
                    rhs_scale=b_planes[4 * br : P, cols],
                    start=True,
                    stop=True,
                )
            e_act[s, c] = work.tile([P, CHUNK], F32, tag="e_act", bufs=4, name="e_act")
            nc.scalar.activation(out=e_act[s, c][:], in_=e_bank[:], func=SILU)

        def result_part(g, c, t):
            if g == 0:
                return f_rows[0][:, t, c * CHUNK : (c + 1) * CHUNK]
            return f_rows[1, c][:, t, :]

        def gate(s, c):
            g, t = s // 4, s % 4
            if g == 1 and t == 0:
                f_rows[1, c] = work.tile([P, PACK, CHUNK], F32, tag="f_rows1", bufs=4, name="f_rows1")
            nc.vector.tensor_tensor(out=result_part(g, c, t), in0=v_bank[s, c][:], in1=e_act[s, c][:], op=MULT)

        out_hbm = out.rearrange("(g p t) f -> g p t f", g=2, t=PACK)
        out_words_hbm = out_words.rearrange("g p m t -> g p (m t)").bitcast(I32)
        out_scales_hbm = out_scales.bitcast(I32)

        def store_rows0(t, c, n):
            cols = slice(c * CHUNK, (c + n) * CHUNK)
            nc.sync.dma_start(out=out_hbm[0][:, t, cols], in_=f_rows[0][:, t, cols])

        def store_rows1(c, t, n):
            cols = slice(c * CHUNK, (c + 1) * CHUNK)
            nc.sync.dma_start(out=out_hbm[1][:, t : t + n, cols], in_=f_rows[1, c][:, t : t + n, :])

        def cast(g, c, engine, lo, hi):
            if (g, c) not in o_groups:
                o_groups[g, c] = work.tile([P, CHUNK, PACK], BF16, tag="o_group", bufs=3, name="o_group", align_bytes=64)
            if g == 0:
                src = f_rows[0][:, :, c * CHUNK + lo : c * CHUNK + hi]
            else:
                src = f_rows[1, c][:, :, lo:hi]
            src = src.rearrange("p t n -> p n t")
            dst = o_groups[g, c][:, lo:hi, :]
            if engine == "v":
                nc.vector.tensor_copy(out=dst, in_=src)
            else:
                nc.scalar.copy(out=dst, in_=src)

        def pack(g, c, lo, hi):
            codes = work.tile([P, hi - lo], U32, tag="o_code", bufs=3, name="o_code", align_bytes=64)
            cols = slice(c * CHUNK + lo, c * CHUNK + hi)
            nc.vector.quantize_mx(
                out=codes[:].bitcast(FP8X4),
                scales=o_scale[g][:, cols],
                in_=o_groups[g, c][:, lo:hi, :].rearrange("p n t -> p (n t)"),
            )
            nc.sync.dma_start(out=out_words_hbm[g][:, cols], in_=codes[:].bitcast(I32))

        def store_scales(g, lo, hi):
            for q in range(4):
                nc.sync.dma_start(
                    out=out_scales_hbm[g, 4 * q : 4 * q + 4, lo // 4 : hi // 4],
                    in_=o_scale[g][32 * q : 32 * q + 4, lo:hi].bitcast(I32),
                )

        turn(0)
        quantize_x(0)
        order_scales(GATE)
        order_channels(GATE)
        hidden(0, GATE)
        order_scales(UP)
        order_channels(UP)
        hidden(0, UP)
        apply_gain(0, GATE)
        turn(1)
        quantize_h(0, GATE)
        apply_gain(0, UP)
        turn(2)
        quantize_h(0, UP)
        quantize_x(1)

        jobs = [(s, br) for s in range(1, 8) for br in (GATE, UP)]
        for i in range(16):
            s, c = i // 4, i % 4
            expand(s, c)
            if i < len(jobs):
                hidden(*jobs[i])
            if i % 2 == 1 and i // 2 + 3 < 8:
                turn(i // 2 + 3)
            if 1 <= i <= len(jobs):
                apply_gain(*jobs[i - 1])
            gate(s, c)
            if 1 <= i <= len(jobs):
                quantize_h(*jobs[i - 1])
            if i % 2 == 0 and i // 2 + 2 < 8:
                quantize_x(i // 2 + 2)
            if c % 2 == 1:
                store_rows0(s, c - 1, 2)

        for c in range(CHUNKS):
            units = [(0, c)] + ([(1, c - 1)] if c else [])
            for t in range(PACK):
                expand(4 + t, c)
                if t // 2 < len(units):
                    u = units[t // 2]
                    lo = V_COLS + (t % 2) * P
                    cast(*u, "s", lo, lo + P)
                    if t % 2 == 0:
                        cast(*u, "v", 0, V_COLS)
                gate(4 + t, c)
                if t // 2 < len(units) and t % 2 == 1:
                    pack(*u, 0, CHUNK)
                if c < 3 and t % 2 == 1:
                    store_rows1(c, t - 1, 2)
                if c == 3:
                    store_rows1(c, t, 1)
        store_scales(0, 0, F)
        store_scales(1, 0, 3 * CHUNK)
        for lo in (0, 256):
            cast(1, 3, "v", lo, lo + P)
            cast(1, 3, "s", lo + P, lo + 2 * P)
            pack(1, 3, lo, lo + 256)
        store_scales(1, 3 * CHUNK, F)
